import numpy as np
import ml_dtypes


def mxq(x, axis, fmt="e4m3"):
    dtype, down = {"e4m3": (ml_dtypes.float8_e4m3fn, 7), "e5m2": (ml_dtypes.float8_e5m2, 14)}[fmt]
    v = np.moveaxis(np.asarray(x, np.float32).astype(ml_dtypes.bfloat16).astype(np.float64), axis, -1)
    blocks = v.reshape(v.shape[:-1] + (-1, 32))
    amax = np.abs(blocks).max(-1, keepdims=True)
    byte = np.maximum(np.where(amax > 0, np.frexp(amax)[1] - 1 + 127, 0) - down, 1)
    scale = np.exp2(byte - 127.0)
    codes = (blocks / scale).astype(np.float32).astype(dtype).astype(np.float64)
    return np.moveaxis((codes * scale).reshape(v.shape), -1, axis)


WIDE = False


def mx_kscale(k):
    if not WIDE:
        return np.ones(k)
    levels = np.array([10, -10, 5, -5, 0])
    if k % 512:
        return np.exp2(np.random.permutation(np.resize(levels, k // 32))).repeat(32)
    a = np.empty((k // 512, 16))
    for p in range(k // 512):
        a[p, :8] = np.random.permutation(np.resize(levels, 8))
        for g in range(8):
            far = levels[np.abs(levels - a[p, g]) >= 10]
            a[p, g + 8] = far[np.random.randint(len(far))]
    return np.exp2(a.ravel()).repeat(32)


def f64(x):
    return np.asarray(x).astype(np.float64)


def striped(idx):
    return np.tile(idx.reshape(-1, 16).T, (8, 1)).astype(np.uint16)


def unstriped(offs):
    return offs[:16].T.reshape(-1).astype(np.int64)


def pack_weight(w):
    k, n = w.shape
    w = f64(np.asarray(w, np.float32).astype(ml_dtypes.bfloat16)).reshape(k // 32, 32, n)
    amax = np.abs(w).max(1)
    byte = np.clip(np.where(amax > 0, np.frexp(amax)[1] - 1 + 127 - 7, 1), 1, 254)
    scaled = (w * np.exp2(127.0 - byte)[:, None, :]).reshape(k, n).astype(np.float32)
    words = np.ascontiguousarray(scaled.reshape(k // 512, 128, 4, n).transpose(0, 1, 3, 2)).astype(ml_dtypes.float8_e4m3fn).view(np.uint8)
    return words, np.ascontiguousarray(byte.astype(np.uint8).reshape(k // 512, 16, n))


def unpack_weight(words, scales):
    g, p, n, _ = words.shape
    vals = np.ascontiguousarray(words).view(ml_dtypes.float8_e4m3fn).astype(np.float64) * np.repeat(np.exp2(scales.astype(np.float64) - 127.0), 8, axis=1)[..., None]
    return vals.transpose(0, 1, 3, 2).reshape(g * 512, n)


K, T, D, S, V, N = 1024, 2048, 3, 1536, 512, 512


def setup_inputs():
    n = np.random.standard_normal
    s = mx_kscale(K)[:, None]
    words, scales = pack_weight(n((K, N)) / np.sqrt(K) / s)
    return {
        "xT": (n((K, T)) * s / np.sqrt(D)).astype(ml_dtypes.bfloat16).astype(np.float32),
        "w_words": words,
        "w_scales": scales,
        "b": (0.3 * n((N, 1))).astype(np.float32),
        "offs": striped(np.concatenate([np.random.permutation(T)[:V] for _ in range(D)])),
    }


def reference(xT, w_words, w_scales, b, offs):
    w = unpack_weight(w_words, w_scales)
    idx = unstriped(offs)
    x = sum(f64(xT)[:, idx[d * V:(d + 1) * V]] for d in range(D))
    return (w.T @ mxq(x, 0, "e4m3")) + f64(b)

from contextlib import ExitStack

import concourse.mybir as mybir

K, T, D, V, N = 1024, 2048, 3, 512, 512
FLOPS = 2 * K * N * V

F32 = mybir.dt.float32
BF16 = mybir.dt.bfloat16
I32 = mybir.dt.int32
U32 = mybir.dt.uint32
U16 = mybir.dt.uint16
U8 = mybir.dt.uint8
FP8X4 = mybir.dt.float8_e4m3fn_x4
ADD = mybir.AluOpType.add
IDENTITY = mybir.ActivationFunctionType.Identity

P = 128
PASSES = K // 512
HALVES = 2
H = V // HALVES
M_TILES = N // P
LIST_ROWS = 16

CHUNKS = [
    [(1024, "s"), (512, "s"), (512, "v")],
    [(1024, "s"), (512, "s"), (512, "s")],
    [(1024, "s"), (512, "s"), (512, "s")],
    [(1024, "s"), (512, "s"), (512, "s")],
]


def tile_picked_hash_lin_bias_sub_l_kernel(tc, xT, w_words, w_scales, b, offs, out):
    nc = tc.nc
    with ExitStack() as ctx:
        keep = ctx.enter_context(tc.tile_pool(name="keep", bufs=1))
        psum = ctx.enter_context(tc.psum_pool(name="psum", bufs=1))

        offsets = keep.tile([P, D * V // LIST_ROWS], U16, name="offsets")
        w_codes = keep.tile([P, PASSES, N], U32, name="w_codes", align_bytes=64)
        w_plane = keep.tile([P, PASSES, N], U8, name="w_plane", align_bytes=64)
        bias = keep.tile([P, M_TILES], F32, name="bias")
        warm = keep.tile([P, 8], F32, name="warm")
        warm_out = keep.tile([P, 8], F32, name="warm_out")

        nc.gpsimd.memset(w_plane[:].rearrange("p a n -> p (a n)").bitcast(U32), 0)
        nc.vector.memset(warm[:], 0.0)
        nc.scalar.activation(warm_out[:], warm[:], IDENTITY, bias=warm[:, 0:1])

        rows = xT.rearrange("(a p u e) c -> a u p e c", p=P, u=2, e=2)
        tables = {}
        for a in range(PASSES):
            for u in range(2):
                table = keep.tile([P, 2, T], F32, name=f"table{a}{u}", align_bytes=64)
                tables[a, u] = table
                c0 = 0
                for width, unused in CHUNKS[2 * a + u]:
                    nc.sync.dma_start(table[:, :, c0 : c0 + width], rows[a, u, :, :, c0 : c0 + width])
                    c0 += width
                if (a, u) == (0, 0):
                    nc.sync.dma_start(offsets[:], offs)
        for a in range(PASSES):
            nc.sync.dma_start(
                w_codes[:, a, :].bitcast(I32), w_words[a].rearrange("p n t -> p (n t)").bitcast(I32)
            )
        scale_rows = w_scales.bitcast(I32).rearrange("a q n -> q a n")
        plane_words = w_plane[:].rearrange("p a n -> p (a n)").bitcast(I32).rearrange("p (a n) -> p a n", a=PASSES)
        for q in range(4):
            nc.sync.dma_start(plane_words[32 * q : 32 * q + 4, :, :], scale_rows[4 * q : 4 * q + 4, :, :])
        with nc.allow_non_contiguous_dma(reason="one bias value a partition"):
            nc.sync.dma_start(bias[:], b.rearrange("(j p) o -> p (j o)", p=P))

        def pack(a, u):
            table = tables[a, u]
            c0 = 0
            for width, engine in CHUNKS[2 * a + u]:
                low = table[:, 1, c0 : c0 + width].bitcast(BF16).rearrange("p (c e) -> p c e", e=2)[:, :, 0]
                if engine == "s":
                    nc.scalar.copy(low, table[:, 0, c0 : c0 + width])
                else:
                    nc.vector.tensor_copy(low, table[:, 0, c0 : c0 + width])
                c0 += width

        def gather(dst, a, u, first, count):
            window = tables[a, u][:, 1, :].bitcast(U32)
            nc.vector.tensor_copy(
                dst, window.indirect(offsets[:, first // LIST_ROWS : (first + count) // LIST_ROWS])
            )

        banks = {}
        for h in range(HALVES):
            for m in range(M_TILES):
                banks[h, m] = psum.tile([P, H], F32, name=f"bank{h}{m}")


        def finish(h, split):
            for m in range(M_TILES):
                result = keep.tile([P, H], F32, name=f"result{h}{m}")
                if split and m % 2 == 1:
                    nc.vector.tensor_scalar_add(result[:], banks[h, m][:], bias[:, m : m + 1])
                else:
                    nc.scalar.activation(result[:], banks[h, m][:], IDENTITY, bias=bias[:, m : m + 1])
                nc.sync.dma_start(out[m * P : (m + 1) * P, h * H : (h + 1) * H], result[:])

        def multiply(a, h, codes, plane):
            for m in range(M_TILES):
                cols = slice(m * P, (m + 1) * P)
                nc.tensor.matmul_mx(
                    out=banks[h, m][:],
                    lhsT=w_codes[:, a, cols].bitcast(FP8X4),
                    lhsT_scale=w_plane[:, a, cols],
                    rhs=codes.bitcast(FP8X4),
                    rhs_scale=plane,
                    start=(a == 0),
                    stop=(a == PASSES - 1),
                )

        x0 = keep.tile([P, V, 2, 2], BF16, name="x0", align_bytes=64)

        def pairs(words):
            return words.bitcast(BF16).rearrange("p (v e) -> p v e", e=2)

        def gather_half(a, u, d, h):
            picked = keep.tile([P, H], U32, name=f"picked{a}{u}{d}{h}", align_bytes=64)
            gather(picked[:], a, u, d * V + h * H, H)
            return picked[:]

        pack(0, 0)
        two = keep.tile([P, 2 * V], U32, name="two00", align_bytes=64)
        third = keep.tile([P, V], U32, name="third00", align_bytes=64)
        partial = keep.tile([P, V, 2], F32, name="partial00", align_bytes=64)
        gather(two[:], 0, 0, 0, 2 * V)
        gather(third[:], 0, 0, 2 * V, V)
        nc.vector.tensor_tensor(partial[:], pairs(two[:, :V]), pairs(two[:, V:]), ADD)
        nc.gpsimd.tensor_tensor(x0[:, :, 0, :], partial[:], pairs(third[:]), ADD)

        pack(0, 1)
        for h, first_adder in ((0, nc.gpsimd), (1, nc.vector)):
            picked = [gather_half(0, 1, d, h) for d in range(D)]
            partial = keep.tile([P, H, 2], F32, name=f"partial01{h}", align_bytes=64)
            first_adder.tensor_tensor(partial[:], pairs(picked[0]), pairs(picked[1]), ADD)
            nc.gpsimd.tensor_tensor(x0[:, h * H : (h + 1) * H, 1, :], partial[:], pairs(picked[2]), ADD)

        partial1 = [keep.tile([P, 2, H, 2], F32, name=f"partial1{h}", align_bytes=64) for h in range(HALVES)]
        third1 = keep.tile([P, 2, V], U32, name="third1", align_bytes=64)
        pack(1, 0)
        gate = keep.tile([P, 8], F32, name="gate", tag="gate", align_bytes=64)
        nc.scalar.copy(gate[:], tables[1, 0][:, 1, T - 8 :])
        two = keep.tile([P, 2 * V], U32, name="two10", align_bytes=64)
        gather(two[:], 1, 0, 0, 2 * V)
        codes0 = keep.tile([P, V], U32, name="codes0", tag="gate", align_bytes=64)
        plane0 = keep.tile([P, V], U8, name="plane0", align_bytes=64)
        nc.vector.quantize_mx(
            out=codes0[:].bitcast(FP8X4), scales=plane0[:], in_=x0[:].rearrange("p v u e -> p (v u e)")
        )
        for h in range(HALVES):
            multiply(0, h, codes0[:, h * H : (h + 1) * H], plane0[:, h * H : (h + 1) * H])
        gather(third1[:, 0, :], 1, 0, 2 * V, V)
        for h in range(HALVES):
            nc.gpsimd.tensor_tensor(
                partial1[h][:, 0], pairs(two[:, h * H : (h + 1) * H]), pairs(two[:, V + h * H : V + (h + 1) * H]), ADD
            )

        pack(1, 1)
        for h in range(HALVES):
            picked = [gather_half(1, 1, d, h) for d in range(2)]
            nc.gpsimd.tensor_tensor(partial1[h][:, 1], pairs(picked[0]), pairs(picked[1]), ADD)
        for h in range(HALVES):
            gather(third1[:, 1, h * H : (h + 1) * H], 1, 1, 2 * V + h * H, H)
        third_values = third1[:].rearrange("p u v -> p (u v)").bitcast(BF16).rearrange("p (u v e) -> p v u e", u=2, e=2)
        Q = H // 2
        for h in range(HALVES):
            x1 = keep.tile([P, H, 2, 2], BF16, name=f"x1{h}", align_bytes=64)
            for c0 in (0, Q):
                nc.vector.tensor_tensor(
                    x1[:, c0 : c0 + Q],
                    partial1[h][:, :, c0 : c0 + Q, :].rearrange("p u v e -> p v u e"),
                    third_values[:, h * H + c0 : h * H + c0 + Q],
                    ADD,
                )
            codes = keep.tile([P, H], U32, name=f"codes1{h}", align_bytes=64)
            plane = keep.tile([P, H], U8, name=f"plane1{h}", align_bytes=64)
            nc.vector.quantize_mx(
                out=codes[:].bitcast(FP8X4), scales=plane[:], in_=x1[:].rearrange("p v u e -> p (v u e)")
            )
            multiply(1, h, codes[:], plane[:])
        finish(0, False)
        finish(1, True)
